import numpy as np
import ml_dtypes


def mxq(x, axis, fmt="e4m3"):
    dtype, down = {"e4m3": (ml_dtypes.float8_e4m3fn, 7), "e5m2": (ml_dtypes.float8_e5m2, 14)}[fmt]
    v = np.moveaxis(np.asarray(x, np.float32).astype(ml_dtypes.bfloat16).astype(np.float64), axis, -1)
    blocks = v.reshape(v.shape[:-1] + (-1, 32))
    amax = np.abs(blocks).max(-1, keepdims=True)
    byte = np.maximum(np.where(amax > 0, np.frexp(amax)[1] - 1 + 127, 0) - down, 1)
    scale = np.exp2(byte - 127.0)
    codes = (blocks / scale).astype(np.float32).astype(dtype).astype(np.float64)
    return np.moveaxis((codes * scale).reshape(v.shape), -1, axis)


WIDE = False


def mx_kscale(k, group=512):
    if not WIDE:
        return np.ones(k)
    levels = np.array([10, -10, 5, -5, 0])
    if group != 512:
        return np.exp2(np.random.permutation(np.resize(levels, k // group))).repeat(group)
    if k % 512:
        return np.exp2(np.random.permutation(np.resize(levels, k // 32))).repeat(32)
    a = np.empty((k // 512, 16))
    for p in range(k // 512):
        a[p, :8] = np.random.permutation(np.resize(levels, 8))
        for g in range(8):
            far = levels[np.abs(levels - a[p, g]) >= 10]
            a[p, g + 8] = far[np.random.randint(len(far))]
    return np.exp2(a.ravel()).repeat(32)


def f64(x):
    return np.asarray(x).astype(np.float64)


def striped(idx):
    return np.tile(np.asarray(idx).reshape(-1, 16).T, (8, 1)).astype(np.uint16)


def unstriped(offs):
    return offs[:16].T.reshape(-1).astype(np.int64)


H, KV, D, NQ, N = 4, 4, 256, 512, 512
CAP = 2.0


def setup_inputs():
    n = np.random.standard_normal
    s = mx_kscale(D, 0)[:, None]
    u = mx_kscale(N)
    t = np.random.uniform(0.5, 2.0, N) * u
    v = n((KV, N, 128))
    v[:, :, 127] = 1.0
    return {
        "qT": (n((H, D, NQ)) * s * (0.70 / np.sqrt(D))).astype(np.float32),
        "kT": (n((KV, D, N)) / s).astype(np.float32),
        "t": t.reshape(N, 1).astype(np.float32),
        "v": (v / t[:, None]).astype(np.float32),
        "og": n((H, NQ, 128)).astype(np.float32),
    }


def reference(qT, kT, t, v, og):
    a = mxq(f64(kT), 1, "e4m3").transpose(0, 2, 1) @ mxq(f64(qT), 1, "e4m3")
    a = CAP * np.tanh(a / CAP)
    p = np.exp(a)
    w = p * f64(t)
    y = mxq(w, 1, "e4m3").transpose(0, 2, 1) @ mxq(f64(v), 1, "e4m3")
    y = y / (y[:, :, 127:128])
    y = y / (1.0 + np.exp(-f64(og)))
    return y

@@ -1,0 +1,300 @@
+from contextlib import ExitStack
+
+import concourse.mybir as mybir
+
+H, D, NQ, N, E = 4, 256, 512, 512, 128
+CAP = 2.0
+FLOPS = 2 * H * NQ * N * (D + E)
+
+F32 = mybir.dt.float32
+BF16 = mybir.dt.bfloat16
+U32 = mybir.dt.uint32
+U8 = mybir.dt.uint8
+FP8X4 = mybir.dt.float8_e4m3fn_x4
+ACT = mybir.ActivationFunctionType
+ALU = mybir.AluOpType
+
+P = 128
+ROWS = 64
+K_SPLIT = 84
+Q_SPLIT = 40
+
+
+def tile_rows_a_exp_cap_gate_kernel(tc, qT, kT, t, v, og, out):
+    nc = tc.nc
+    with ExitStack() as ctx:
+        sb = ctx.enter_context(tc.tile_pool(name="sb", bufs=1))
+        ps = ctx.enter_context(tc.psum_pool(name="ps", bufs=1))
+
+        def tiles(name, count, shape, dtype):
+            return [sb.tile(shape, dtype, name="%s%d" % (name, i), align_bytes=64) for i in range(count)]
+
+        k_raw = tiles("k_raw", 2, [P, 4, N], F32)
+        q_raw0 = tiles("q_raw_first", 2, [P, 4, 256], F32)
+        q_raw1 = tiles("q_raw_second", 1, [P, 4, NQ], F32)[0]
+        v_raw = tiles("v_raw", 2, [P, 2, 4, E], F32)
+        og_raw = tiles("og_raw", 2, [P, 4, 256], F32)
+        t_sb = tiles("t_sb", 1, [P, 4], F32)[0]
+        k_bf = tiles("k_bf", 2, [P, 4, 128, 4], BF16)
+        q_bf = tiles("q_bf", 4, [P, 2, 128, 4], BF16)
+        v_bf = tiles("v_bf", 2, [P, 2, E, 4], BF16)
+        k_codes = tiles("k_codes", 2, [P, 512], U32)
+        k_scales = tiles("k_scales", 2, [P, 512], U8)
+        q_codes = tiles("q_codes", 4, [P, 256], U32)
+        q_scales = tiles("q_scales", 4, [P, 256], U8)
+        v_codes = tiles("v_codes", 2, [P, 256], U32)
+        v_scales = tiles("v_scales", 2, [P, 256], U8)
+        capped = tiles("capped", 8, [P, 2, 128, 4], F32)
+        probs = tiles("probs", 8, [P, 256, 4], F32)
+        w_bf = tiles("w_bf", 8, [P, 256, 4], BF16)
+        w_codes = tiles("w_codes", 8, [P, 256], U32)
+        w_scales = tiles("w_scales", 8, [P, 256], U8)
+        gate_t = tiles("gate_t", 3, [P, 4, 256], F32)
+        gate = tiles("gate", 3, [P, 4, 256], F32)
+        recip = tiles("recip", 8, [P, 2, 1], F32)
+        res = tiles("res", 8, [P, 2, E], F32)
+        score = [[ps.tile([P, 4, 128], F32, name="score%d%d" % (g, b)) for b in range(2)] for g in range(2)]
+        y = [ps.tile([P, 2, E], F32, name="y%d" % i) for i in range(4)]
+
+        def head(u):
+            return 2 * (u // 4) + u % 2
+
+        def half(u):
+            return (u // 2) % 2
+
+        def pair_rows(x, pair):
+            return x[2 * pair : 2 * pair + 2].rearrange("g (p j) n -> (g p) j n", j=4)
+
+        def q_src(pair, a):
+            if pair == 0:
+                return q_raw0[a][:]
+            return q_raw1[:, :, 256 * a : 256 * a + 256]
+
+        def k_copy(eng, pair, s0, s1):
+            o = k_bf[pair][:].rearrange("p r s j -> p s j r")[:, s0:s1]
+            i = k_raw[pair][:].rearrange("p j (s r) -> p s j r", r=4)[:, s0:s1]
+            if eng == "v":
+                nc.vector.tensor_copy(out=o, in_=i)
+            else:
+                nc.scalar.activation(out=o, in_=i, func=ACT.Copy)
+
+        def q_copy(eng, pair, a, c0, c1):
+            o = q_bf[2 * pair + a][:].rearrange("p b (c i) j -> p c j i b", i=2)[:, c0:c1]
+            i = q_src(pair, a).rearrange("p j (c i b) -> p c j i b", i=2, b=2)[:, c0:c1]
+            if eng == "v":
+                nc.vector.tensor_copy(out=o, in_=i)
+            else:
+                nc.scalar.copy(out=o, in_=i)
+
+        def q_first(b):
+            nc.scalar.copy(
+                out=q_bf[0][:, b].rearrange("p (c i) j -> p c j i", i=2),
+                in_=q_raw0[0][:].rearrange("p j (c i b) -> p b c j i", i=2, b=2)[:, b],
+            )
+            cols = slice(128 * b, 128 * b + 128)
+            nc.vector.quantize_mx(
+                out=q_codes[0][:, cols].bitcast(FP8X4),
+                scales=q_scales[0][:, cols],
+                in_=q_bf[0][:, b].rearrange("p m j -> p (m j)"),
+            )
+
+        def v_copy(pair):
+            nc.vector.tensor_copy(
+                out=v_bf[pair][:].rearrange("p g (c i) j -> p g c j i", i=4),
+                in_=v_raw[pair][:].rearrange("p g j (c i) -> p g c j i", i=4),
+            )
+
+        def quant(codes, scales, src):
+            nc.vector.quantize_mx(out=codes[:].bitcast(FP8X4), scales=scales[:], in_=src)
+
+        def k_quant(pair):
+            quant(k_codes[pair], k_scales[pair], k_bf[pair][:].rearrange("p r s j -> p (r s j)"))
+
+        def q_quant(pair, a):
+            i = 2 * pair + a
+            quant(q_codes[i], q_scales[i], q_bf[i][:].rearrange("p b m j -> p (b m j)"))
+
+        def v_quant(pair):
+            quant(v_codes[pair], v_scales[pair], v_bf[pair][:].rearrange("p g e j -> p (g e j)"))
+
+        def scores(u, b):
+            pair, g = u // 4, u % 2
+            rows = slice(ROWS * g, ROWS * g + ROWS)
+            qi = 2 * pair + half(u)
+            qc = slice(128 * b, 128 * b + 128)
+            for r in range(4):
+                kc = slice(128 * r, 128 * r + 128)
+                nc.tensor.matmul_mx(
+                    out=score[g][b][:, r, :],
+                    lhsT=k_codes[pair][rows, kc].bitcast(FP8X4),
+                    lhsT_scale=k_scales[pair][rows, kc],
+                    rhs=q_codes[qi][rows, qc].bitcast(FP8X4),
+                    rhs_scale=q_scales[qi][rows, qc],
+                    start=True,
+                    stop=True,
+                )
+
+        def cap(u, b):
+            nc.scalar.activation(
+                out=capped[u][:, b],
+                in_=score[u % 2][b][:].rearrange("p r m -> p m r"),
+                func=ACT.Tanh,
+                scale=1.0 / CAP,
+            )
+
+        def expo(u):
+            nc.scalar.activation(
+                out=probs[u][:].rearrange("p q r -> p (q r)"),
+                in_=capped[u][:].rearrange("p b m r -> p (b m r)"),
+                func=ACT.Exp,
+                scale=CAP,
+            )
+
+        def weigh(u):
+            nc.vector.tensor_tensor(
+                out=w_bf[u][:],
+                in0=probs[u][:],
+                in1=t_sb[:].unsqueeze(1).to_broadcast([P, 256, 4]),
+                op=ALU.mult,
+            )
+
+        def w_quant(u):
+            quant(w_codes[u], w_scales[u], w_bf[u][:].rearrange("p q r -> p (q r)"))
+
+        def values(u):
+            pair, g = u // 4, u % 2
+            vc = slice(128 * g, 128 * g + 128)
+            for b in range(2):
+                wc = slice(128 * b, 128 * b + 128)
+                nc.tensor.matmul_mx(
+                    out=y[u % 4][:, b, :],
+                    lhsT=w_codes[u][:, wc].bitcast(FP8X4),
+                    lhsT_scale=w_scales[u][:, wc],
+                    rhs=v_codes[pair][:, vc].bitcast(FP8X4),
+                    rhs_scale=v_scales[pair][:, vc],
+                    start=True,
+                    stop=True,
+                )
+
+        def gate_view(x, grp):
+            if grp == 0:
+                return x[:]
+            return x[:].rearrange("p (g a) c -> p a g c", a=2)[:, grp - 1]
+
+        def gate_tanh(grp):
+            nc.scalar.activation(
+                out=gate_view(gate_t[grp], grp), in_=gate_view(og_raw[min(grp, 1)], grp), func=ACT.Tanh, scale=0.5
+            )
+
+        def gate_fin(grp, eng):
+            if eng == "v":
+                nc.vector.tensor_scalar(
+                    out=gate_view(gate[grp], grp), in0=gate_view(gate_t[grp], grp),
+                    scalar1=0.5, scalar2=0.5, op0=ALU.mult, op1=ALU.add,
+                )
+            else:
+                nc.scalar.activation(
+                    out=gate_view(gate[grp], grp), in_=gate_view(gate_t[grp], grp), func=ACT.Copy, scale=0.5, bias=0.5
+                )
+
+        def inv(u):
+            nc.vector.reciprocal(out=recip[u][:], in_=y[u % 4][:, :, E - 1 : E])
+
+        def finish(u):
+            grp = 0 if u < 4 else 1 + half(u)
+            gi = 2 * (u % 2) + half(u)
+            for b in range(2):
+                nc.vector.scalar_tensor_tensor(
+                    out=res[u][:, b, :],
+                    in0=y[u % 4][:, b, :],
+                    scalar=recip[u][:, b, :],
+                    in1=gate[grp][:, gi, E * b : E * b + E],
+                    op0=ALU.mult,
+                    op1=ALU.mult,
+                )
+            nc.sync.dma_start(
+                out=out[head(u)].rearrange("(a m b) e -> a m (b e)", a=2, b=2)[half(u)],
+                in_=res[u][:].rearrange("p b e -> p (b e)"),
+            )
+
+        def v_rows(pair):
+            return v[2 * pair : 2 * pair + 2].rearrange("g (p j) e -> p g (j e)", j=4)
+
+        def og_rows(pair):
+            return og[2 * pair : 2 * pair + 2].rearrange("g (a m b) e -> m (g a) (b e)", a=2, b=2)
+
+        with tc.manual_schedule():
+            nc.sync.dma_start(out=k_raw[0][:], in_=pair_rows(kT, 0))
+            nc.sync.dma_start(out=q_raw0[0][:], in_=pair_rows(qT, 0)[:, :, 0:256])
+            nc.sync.dma_start(out=q_raw0[1][:], in_=pair_rows(qT, 0)[:, :, 256:512])
+            nc.sync.dma_start(out=t_sb[:], in_=t.rearrange("(p j) o -> p (j o)", j=4))
+            nc.sync.dma_start(out=k_raw[1][:], in_=pair_rows(kT, 1))
+            nc.sync.dma_start(out=v_raw[0][:].rearrange("p g j e -> p g (j e)"), in_=v_rows(0))
+            nc.sync.dma_start(out=q_raw1[:], in_=pair_rows(qT, 1))
+            nc.sync.dma_start(out=og_raw[0][:], in_=og_rows(0))
+            nc.sync.dma_start(out=v_raw[1][:].rearrange("p g j e -> p g (j e)"), in_=v_rows(1))
+            nc.sync.dma_start(out=og_raw[1][:], in_=og_rows(1))
+
+            k_copy("v", 0, 0, K_SPLIT)
+            k_copy("s", 0, K_SPLIT, 128)
+            k_quant(0)
+            q_first(0)
+            scores(0, 0)
+            q_first(1)
+            scores(0, 1)
+            scores(1, 0)
+            scores(1, 1)
+            q_copy("v", 0, 1, 0, 64)
+            q_quant(0, 1)
+            k_copy("v", 1, 0, 128)
+            v_copy(0)
+            k_quant(1)
+
+            cap(0, 0)
+            cap(0, 1)
+            before = {
+                0: [lambda: v_quant(0)],
+                1: [lambda: q_copy("v", 1, 0, 0, 64)],
+                2: [lambda: q_copy("v", 1, 1, 0, 64)],
+                3: [lambda: gate_fin(0, "v"), lambda: inv(0), lambda: inv(1)],
+                4: [lambda: v_quant(1), lambda: inv(2), lambda: inv(3)],
+                5: [lambda: gate_fin(1, "v")],
+                6: [lambda: inv(4)],
+                7: [lambda: inv(5), lambda: finish(5), lambda: inv(6)],
+            }
+            after = {
+                0: [],
+                1: [lambda: q_quant(1, 0)],
+                2: [lambda: q_quant(1, 1)],
+                3: [lambda: finish(0), lambda: v_copy(1), lambda: finish(1)],
+                4: [lambda: finish(2), lambda: finish(3)],
+                5: [],
+                6: [lambda: finish(4)],
+                7: [lambda: finish(6), lambda: inv(7), lambda: finish(7)],
+            }
+            for u in range(8):
+                if u + 1 < 8:
+                    cap(u + 1, 0)
+                expo(u)
+                if u == 2:
+                    gate_tanh(0)
+                if u == 4:
+                    gate_tanh(1)
+                if u == 7:
+                    gate_tanh(2)
+                    gate_fin(2, "s")
+                if u + 1 < 8:
+                    cap(u + 1, 1)
+                if u + 2 < 8:
+                    scores(u + 2, 0)
+                    scores(u + 2, 1)
+                if u > 0:
+                    values(u - 1)
+                weigh(u)
+                for step in before[u]:
+                    step()
+                w_quant(u)
+                if u == 7:
+                    values(u)
+                for step in after[u]:
+                    step()

@@ -30,8 +30,7 @@ def tile_rows_a_exp_cap_gate_kernel(tc, qT, kT, t, v, og, out):
             return [sb.tile(shape, dtype, name="%s%d" % (name, i), align_bytes=64) for i in range(count)]
 
         k_raw = tiles("k_raw", 2, [P, 4, N], F32)
-        q_raw0 = tiles("q_raw_first", 2, [P, 4, 256], F32)
-        q_raw1 = tiles("q_raw_second", 1, [P, 4, NQ], F32)[0]
+        q_raw = tiles("q_raw", 4, [P, 4, 256], F32)
         v_raw = tiles("v_raw", 2, [P, 2, 4, E], F32)
         og_raw = tiles("og_raw", 2, [P, 4, 256], F32)
         t_sb = tiles("t_sb", 1, [P, 4], F32)[0]
@@ -49,8 +48,8 @@ def tile_rows_a_exp_cap_gate_kernel(tc, qT, kT, t, v, og, out):
         w_bf = tiles("w_bf", 8, [P, 256, 4], BF16)
         w_codes = tiles("w_codes", 8, [P, 256], U32)
         w_scales = tiles("w_scales", 8, [P, 256], U8)
-        gate_t = tiles("gate_t", 3, [P, 4, 256], F32)
-        gate = tiles("gate", 3, [P, 4, 256], F32)
+        gate_t = tiles("gate_t", 2, [P, 4, 256], F32)
+        gate = tiles("gate", 2, [P, 4, 256], F32)
         recip = tiles("recip", 8, [P, 2, 1], F32)
         res = tiles("res", 8, [P, 2, E], F32)
         score = [[ps.tile([P, 4, 128], F32, name="score%d%d" % (g, b)) for b in range(2)] for g in range(2)]
@@ -66,17 +65,16 @@ def tile_rows_a_exp_cap_gate_kernel(tc, qT, kT, t, v, og, out):
             return x[2 * pair : 2 * pair + 2].rearrange("g (p j) n -> (g p) j n", j=4)
 
         def q_src(pair, a):
-            if pair == 0:
-                return q_raw0[a][:]
-            return q_raw1[:, :, 256 * a : 256 * a + 256]
+            return q_raw[2 * pair + a][:]
 
         def k_copy(eng, pair, s0, s1):
-            o = k_bf[pair][:].rearrange("p r s j -> p s j r")[:, s0:s1]
-            i = k_raw[pair][:].rearrange("p j (s r) -> p s j r", r=4)[:, s0:s1]
+            o = k_bf[pair][:].rearrange("p (u x) s j -> p u s j x", x=2)[:, :, s0:s1]
+            i = k_raw[pair][:].rearrange("p j (s u x) -> p u s j x", u=2, x=2)[:, :, s0:s1]
             if eng == "v":
                 nc.vector.tensor_copy(out=o, in_=i)
             else:
-                nc.scalar.activation(out=o, in_=i, func=ACT.Copy)
+                for u in range(2):
+                    nc.scalar.activation(out=o[:, u], in_=i[:, u], func=ACT.Copy)
 
         def q_copy(eng, pair, a, c0, c1):
             o = q_bf[2 * pair + a][:].rearrange("p b (c i) j -> p c j i b", i=2)[:, c0:c1]
@@ -86,11 +84,13 @@ def tile_rows_a_exp_cap_gate_kernel(tc, qT, kT, t, v, og, out):
             else:
                 nc.scalar.copy(out=o, in_=i)
 
-        def q_first(b):
+        def q_first_copy(b):
             nc.scalar.copy(
                 out=q_bf[0][:, b].rearrange("p (c i) j -> p c j i", i=2),
-                in_=q_raw0[0][:].rearrange("p j (c i b) -> p b c j i", i=2, b=2)[:, b],
+                in_=q_raw[0][:].rearrange("p j (c i b) -> p b c j i", i=2, b=2)[:, b],
             )
+
+        def q_first_quant(b):
             cols = slice(128 * b, 128 * b + 128)
             nc.vector.quantize_mx(
                 out=q_codes[0][:, cols].bitcast(FP8X4),
@@ -142,32 +142,40 @@ def tile_rows_a_exp_cap_gate_kernel(tc, qT, kT, t, v, og, out):
                 scale=1.0 / CAP,
             )
 
-        def expo(u):
+        def expo(u, b0=0, b1=2):
             nc.scalar.activation(
-                out=probs[u][:].rearrange("p q r -> p (q r)"),
-                in_=capped[u][:].rearrange("p b m r -> p (b m r)"),
+                out=probs[u][:, 128 * b0 : 128 * b1].rearrange("p q r -> p (q r)"),
+                in_=capped[u][:, b0:b1].rearrange("p b m r -> p (b m r)"),
                 func=ACT.Exp,
                 scale=CAP,
             )
 
-        def weigh(u):
+        def weigh(u, b0=0, b1=2):
             nc.vector.tensor_tensor(
-                out=w_bf[u][:],
-                in0=probs[u][:],
-                in1=t_sb[:].unsqueeze(1).to_broadcast([P, 256, 4]),
+                out=w_bf[u][:, 128 * b0 : 128 * b1],
+                in0=probs[u][:, 128 * b0 : 128 * b1],
+                in1=t_sb[:].unsqueeze(1).to_broadcast([P, 128 * (b1 - b0), 4]),
                 op=ALU.mult,
             )
 
-        def w_quant(u):
-            quant(w_codes[u], w_scales[u], w_bf[u][:].rearrange("p q r -> p (q r)"))
+        def w_quant(u, b0=0, b1=2):
+            cols = slice(128 * b0, 128 * b1)
+            nc.vector.quantize_mx(
+                out=w_codes[u][:, cols].bitcast(FP8X4),
+                scales=w_scales[u][:, cols],
+                in_=w_bf[u][:, cols].rearrange("p q r -> p (q r)"),
+            )
 
-        def values(u):
+        def bank(u, b):
+            return y[0] if (u, b) == (7, 1) else y[u % 4]
+
+        def values(u, b0=0, b1=2):
             pair, g = u // 4, u % 2
             vc = slice(128 * g, 128 * g + 128)
-            for b in range(2):
+            for b in range(b0, b1):
                 wc = slice(128 * b, 128 * b + 128)
                 nc.tensor.matmul_mx(
-                    out=y[u % 4][:, b, :],
+                    out=bank(u, b)[:, b, :],
                     lhsT=w_codes[u][:, wc].bitcast(FP8X4),
                     lhsT_scale=w_scales[u][:, wc],
                     rhs=v_codes[pair][:, vc].bitcast(FP8X4),
@@ -176,46 +184,47 @@ def tile_rows_a_exp_cap_gate_kernel(tc, qT, kT, t, v, og, out):
                     stop=True,
                 )
 
-        def gate_view(x, grp):
-            if grp == 0:
-                return x[:]
-            return x[:].rearrange("p (g a) c -> p a g c", a=2)[:, grp - 1]
+        def gate_view(x, units):
+            u = units[0]
+            full = x[u // 4][:]
+            if len(units) == 4:
+                return full
+            if len(units) == 2:
+                return full.rearrange("p (g a) c -> p a g c", a=2)[:, half(u)]
+            return full[:, 2 * (u % 2) + half(u)]
 
-        def gate_tanh(grp):
-            nc.scalar.activation(
-                out=gate_view(gate_t[grp], grp), in_=gate_view(og_raw[min(grp, 1)], grp), func=ACT.Tanh, scale=0.5
-            )
+        def gate_tanh(units):
+            nc.scalar.activation(out=gate_view(gate_t, units), in_=gate_view(og_raw, units), func=ACT.Tanh, scale=0.5)
 
-        def gate_fin(grp, eng):
+        def gate_fin(units, eng):
             if eng == "v":
                 nc.vector.tensor_scalar(
-                    out=gate_view(gate[grp], grp), in0=gate_view(gate_t[grp], grp),
+                    out=gate_view(gate, units), in0=gate_view(gate_t, units),
                     scalar1=0.5, scalar2=0.5, op0=ALU.mult, op1=ALU.add,
                 )
             else:
                 nc.scalar.activation(
-                    out=gate_view(gate[grp], grp), in_=gate_view(gate_t[grp], grp), func=ACT.Copy, scale=0.5, bias=0.5
+                    out=gate_view(gate, units), in_=gate_view(gate_t, units), func=ACT.Copy, scale=0.5, bias=0.5
                 )
 
-        def inv(u):
-            nc.vector.reciprocal(out=recip[u][:], in_=y[u % 4][:, :, E - 1 : E])
+        def inv(u, b0=0, b1=2):
+            nc.vector.reciprocal(out=recip[u][:, b0:b1], in_=bank(u, b0)[:, b0:b1, E - 1 : E])
 
-        def finish(u):
-            grp = 0 if u < 4 else 1 + half(u)
-            gi = 2 * (u % 2) + half(u)
-            for b in range(2):
+        def finish(u, b0=0, b1=2):
+            for b in range(b0, b1):
                 nc.vector.scalar_tensor_tensor(
                     out=res[u][:, b, :],
-                    in0=y[u % 4][:, b, :],
+                    in0=bank(u, b)[:, b, :],
                     scalar=recip[u][:, b, :],
-                    in1=gate[grp][:, gi, E * b : E * b + E],
+                    in1=gate_view(gate, [u])[:, E * b : E * b + E],
                     op0=ALU.mult,
                     op1=ALU.mult,
                 )
-            nc.sync.dma_start(
-                out=out[head(u)].rearrange("(a m b) e -> a m (b e)", a=2, b=2)[half(u)],
-                in_=res[u][:].rearrange("p b e -> p (b e)"),
-            )
+            if b1 == 2:
+                nc.sync.dma_start(
+                    out=out[head(u)].rearrange("(a m b) e -> a m (b e)", a=2, b=2)[half(u)],
+                    in_=res[u][:].rearrange("p b e -> p (b e)"),
+                )
 
         def v_rows(pair):
             return v[2 * pair : 2 * pair + 2].rearrange("g (p j) e -> p g (j e)", j=4)
@@ -225,76 +234,132 @@ def tile_rows_a_exp_cap_gate_kernel(tc, qT, kT, t, v, og, out):
 
         with tc.manual_schedule():
             nc.sync.dma_start(out=k_raw[0][:], in_=pair_rows(kT, 0))
-            nc.sync.dma_start(out=q_raw0[0][:], in_=pair_rows(qT, 0)[:, :, 0:256])
-            nc.sync.dma_start(out=q_raw0[1][:], in_=pair_rows(qT, 0)[:, :, 256:512])
+            nc.sync.dma_start(out=q_raw[0][:], in_=pair_rows(qT, 0)[:, :, 0:256])
+            nc.sync.dma_start(out=q_raw[1][:], in_=pair_rows(qT, 0)[:, :, 256:512])
             nc.sync.dma_start(out=t_sb[:], in_=t.rearrange("(p j) o -> p (j o)", j=4))
-            nc.sync.dma_start(out=k_raw[1][:], in_=pair_rows(kT, 1))
             nc.sync.dma_start(out=v_raw[0][:].rearrange("p g j e -> p g (j e)"), in_=v_rows(0))
-            nc.sync.dma_start(out=q_raw1[:], in_=pair_rows(qT, 1))
+            nc.sync.dma_start(out=q_raw[2][:], in_=pair_rows(qT, 1)[:, :, 0:256])
+            nc.sync.dma_start(out=k_raw[1][:], in_=pair_rows(kT, 1))
             nc.sync.dma_start(out=og_raw[0][:], in_=og_rows(0))
-            nc.sync.dma_start(out=v_raw[1][:].rearrange("p g j e -> p g (j e)"), in_=v_rows(1))
+            nc.sync.dma_start(out=q_raw[3][:], in_=pair_rows(qT, 1)[:, :, 256:512])
             nc.sync.dma_start(out=og_raw[1][:], in_=og_rows(1))
-
+            nc.sync.dma_start(out=v_raw[1][:].rearrange("p g j e -> p g (j e)"), in_=v_rows(1))
             k_copy("v", 0, 0, K_SPLIT)
             k_copy("s", 0, K_SPLIT, 128)
             k_quant(0)
-            q_first(0)
+            q_first_copy(0)
+            q_first_copy(1)
+            q_first_quant(0)
             scores(0, 0)
-            q_first(1)
+            q_first_quant(1)
             scores(0, 1)
             scores(1, 0)
             scores(1, 1)
             q_copy("v", 0, 1, 0, 64)
-            q_quant(0, 1)
-            k_copy("v", 1, 0, 128)
             v_copy(0)
-            k_quant(1)
-
+            q_quant(0, 1)
+            v_quant(0)
+            q_copy("v", 1, 0, 0, 64)
             cap(0, 0)
             cap(0, 1)
-            before = {
-                0: [lambda: v_quant(0)],
-                1: [lambda: q_copy("v", 1, 0, 0, 64)],
-                2: [lambda: q_copy("v", 1, 1, 0, 64)],
-                3: [lambda: gate_fin(0, "v"), lambda: inv(0), lambda: inv(1)],
-                4: [lambda: v_quant(1), lambda: inv(2), lambda: inv(3)],
-                5: [lambda: gate_fin(1, "v")],
-                6: [lambda: inv(4)],
-                7: [lambda: inv(5), lambda: finish(5), lambda: inv(6)],
-            }
-            after = {
-                0: [],
-                1: [lambda: q_quant(1, 0)],
-                2: [lambda: q_quant(1, 1)],
-                3: [lambda: finish(0), lambda: v_copy(1), lambda: finish(1)],
-                4: [lambda: finish(2), lambda: finish(3)],
-                5: [],
-                6: [lambda: finish(4)],
-                7: [lambda: finish(6), lambda: inv(7), lambda: finish(7)],
-            }
-            for u in range(8):
-                if u + 1 < 8:
-                    cap(u + 1, 0)
-                expo(u)
-                if u == 2:
-                    gate_tanh(0)
-                if u == 4:
-                    gate_tanh(1)
-                if u == 7:
-                    gate_tanh(2)
-                    gate_fin(2, "s")
-                if u + 1 < 8:
-                    cap(u + 1, 1)
-                if u + 2 < 8:
-                    scores(u + 2, 0)
-                    scores(u + 2, 1)
-                if u > 0:
-                    values(u - 1)
-                weigh(u)
-                for step in before[u]:
-                    step()
-                w_quant(u)
-                if u == 7:
-                    values(u)
-                for step in after[u]:
-                    step()
+            expo(0, 0, 1)
+            cap(1, 0)
+            expo(0, 1, 2)
+            cap(1, 1)
+            scores(2, 0)
+            scores(2, 1)
+            weigh(0, 0, 1)
+            q_quant(1, 0)
+            weigh(0, 1, 2)
+            k_copy("v", 1, 0, 128)
+            w_quant(0)
+            k_quant(1)
+            cap(2, 0)
+            expo(1)
+            cap(2, 1)
+            gate_tanh([0, 1])
+            scores(3, 0)
+            scores(3, 1)
+            values(0)
+            weigh(1)
+            q_copy("v", 1, 1, 0, 64)
+            w_quant(1)
+            q_quant(1, 1)
+            gate_fin([0, 1], "v")
+            inv(0)
+            cap(3, 0)
+            expo(2)
+            cap(3, 1)
+            gate_tanh([2, 3])
+            scores(4, 0)
+            scores(4, 1)
+            values(1)
+            weigh(2)
+            inv(1)
+            finish(0)
+            w_quant(2)
+            finish(1)
+            v_copy(1)
+            gate_fin([2, 3], "v")
+            cap(4, 0)
+            expo(3)
+            cap(4, 1)
+            gate_tanh([4, 5])
+            scores(5, 0)
+            scores(5, 1)
+            values(2)
+            weigh(3)
+            inv(2)
+            v_quant(1)
+            w_quant(3)
+            finish(2)
+            cap(5, 0)
+            expo(4)
+            cap(5, 1)
+            scores(6, 0)
+            scores(6, 1)
+            values(3)
+            weigh(4)
+            inv(3)
+            gate_fin([4, 5], "v")
+            w_quant(4)
+            finish(3)
+            cap(6, 0)
+            expo(5)
+            cap(6, 1)
+            scores(7, 0)
+            scores(7, 1)
+            values(4)
+            weigh(5)
+            inv(4)
+            w_quant(5)
+            finish(4)
+            expo(6, 0, 1)
+            cap(7, 0)
+            expo(6, 1, 2)
+            cap(7, 1)
+            values(5)
+            expo(7, 0, 1)
+            expo(7, 1, 2)
+            gate_tanh([6])
+            gate_tanh([7])
+            gate_fin([6], "s")
+            gate_fin([7], "s")
+            weigh(6, 0, 1)
+            inv(5)
+            weigh(6, 1, 2)
+            finish(5)
+            w_quant(6)
+            values(6)
+            weigh(7, 0, 1)
+            weigh(7, 1, 2)
+            w_quant(7, 0, 1)
+            values(7, 0, 1)
+            inv(6)
+            w_quant(7, 1, 2)
+            values(7, 1, 2)
+            finish(6)
+            inv(7, 0, 1)
+            inv(7, 1, 2)
+            finish(7, 0, 1)
+            finish(7, 1, 2)

@@ -17,7 +17,6 @@ ALU = mybir.AluOpType
 P = 128
 ROWS = 64
 K_SPLIT = 84
-Q_SPLIT = 40
 
 
 def tile_rows_a_exp_cap_gate_kernel(tc, qT, kT, t, v, og, out):
@@ -29,18 +28,20 @@ def tile_rows_a_exp_cap_gate_kernel(tc, qT, kT, t, v, og, out):
         def tiles(name, count, shape, dtype):
             return [sb.tile(shape, dtype, name="%s%d" % (name, i), align_bytes=64) for i in range(count)]
 
+        q_parts = [(0, 1), (1, 4), (4, 8)]
         k_raw = tiles("k_raw", 2, [P, 4, N], F32)
-        q_raw = tiles("q_raw", 4, [P, 4, 256], F32)
+        q_raw = {}
+        for part in q_parts:
+            q_raw[part] = sb.tile([P, 4, 128 * (part[1] - part[0])], F32, name="q_raw%d" % part[0], align_bytes=64)
         v_raw = tiles("v_raw", 2, [P, 2, 4, E], F32)
-        og_raw = tiles("og_raw", 2, [P, 4, 256], F32)
         t_sb = tiles("t_sb", 1, [P, 4], F32)[0]
         k_bf = tiles("k_bf", 2, [P, 4, 128, 4], BF16)
-        q_bf = tiles("q_bf", 4, [P, 2, 128, 4], BF16)
+        q_bf = tiles("q_bf", 1, [P, 1024, 4], BF16)[0]
         v_bf = tiles("v_bf", 2, [P, 2, E, 4], BF16)
         k_codes = tiles("k_codes", 2, [P, 512], U32)
         k_scales = tiles("k_scales", 2, [P, 512], U8)
-        q_codes = tiles("q_codes", 4, [P, 256], U32)
-        q_scales = tiles("q_scales", 4, [P, 256], U8)
+        q_codes = tiles("q_codes", 1, [P, 1024], U32)[0]
+        q_scales = tiles("q_scales", 1, [P, 1024], U8)[0]
         v_codes = tiles("v_codes", 2, [P, 256], U32)
         v_scales = tiles("v_scales", 2, [P, 256], U8)
         capped = tiles("capped", 8, [P, 2, 128, 4], F32)
@@ -48,24 +49,41 @@ def tile_rows_a_exp_cap_gate_kernel(tc, qT, kT, t, v, og, out):
         w_bf = tiles("w_bf", 8, [P, 256, 4], BF16)
         w_codes = tiles("w_codes", 8, [P, 256], U32)
         w_scales = tiles("w_scales", 8, [P, 256], U8)
-        gate_t = tiles("gate_t", 2, [P, 4, 256], F32)
-        gate = tiles("gate", 2, [P, 4, 256], F32)
         recip = tiles("recip", 8, [P, 2, 1], F32)
         res = tiles("res", 8, [P, 2, E], F32)
         score = [[ps.tile([P, 4, 128], F32, name="score%d%d" % (g, b)) for b in range(2)] for g in range(2)]
         y = [ps.tile([P, 2, E], F32, name="y%d" % i) for i in range(4)]
 
-        def head(u):
-            return 2 * (u // 4) + u % 2
-
-        def half(u):
-            return (u // 2) % 2
-
         def pair_rows(x, pair):
             return x[2 * pair : 2 * pair + 2].rearrange("g (p j) n -> (g p) j n", j=4)
 
-        def q_src(pair, a):
-            return q_raw[2 * pair + a][:]
+        def load_k(pair):
+            nc.sync.dma_start(out=k_raw[pair][:], in_=pair_rows(kT, pair))
+
+        def load_q(i):
+            u0, u1 = q_parts[i]
+            c0 = 128 * (u0 % 4)
+            nc.sync.dma_start(out=q_raw[q_parts[i]][:], in_=pair_rows(qT, u0 // 4)[:, :, c0 : c0 + 128 * (u1 - u0)])
+
+        def load_t():
+            nc.sync.dma_start(out=t_sb[:], in_=t.rearrange("(p j) o -> p (j o)", j=4))
+
+        def load_v(pair):
+            nc.sync.dma_start(
+                out=v_raw[pair][:].rearrange("p g j e -> p g (j e)"),
+                in_=v[2 * pair : 2 * pair + 2].rearrange("g (p j) e -> p g (j e)", j=4),
+            )
+
+        def load_og(pair):
+            for g in range(2):
+                nc.sync.dma_start(
+                    out=og_all[pair][:, :, g, :],
+                    in_=og[2 * pair + g].rearrange("(b m) e -> m b e", b=4),
+                )
+
+        og_all = tiles("og_all", 2, [P, 4, 2, E], F32)
+        gt_all = tiles("gt_all", 2, [P, 4, 2, E], F32)
+        g_all = tiles("g_all", 2, [P, 4, 2, E], F32)
 
         def k_copy(eng, pair, s0, s1):
             o = k_bf[pair][:].rearrange("p (u x) s j -> p u s j x", x=2)[:, :, s0:s1]
@@ -76,27 +94,15 @@ def tile_rows_a_exp_cap_gate_kernel(tc, qT, kT, t, v, og, out):
                 for u in range(2):
                     nc.scalar.activation(out=o[:, u], in_=i[:, u], func=ACT.Copy)
 
-        def q_copy(eng, pair, a, c0, c1):
-            o = q_bf[2 * pair + a][:].rearrange("p b (c i) j -> p c j i b", i=2)[:, c0:c1]
-            i = q_src(pair, a).rearrange("p j (c i b) -> p c j i b", i=2, b=2)[:, c0:c1]
+        def q_copy(eng, u0, u1):
+            part = [x for x in q_parts if x[0] <= u0 and u1 <= x[1]][0]
+            src = q_raw[part][:, :, 128 * (u0 - part[0]) : 128 * (u1 - part[0])]
+            o = q_bf[:, 128 * u0 : 128 * u1].rearrange("p (c i) j -> p c j i", i=4)
+            i = src.rearrange("p j (c i) -> p c j i", i=4)
             if eng == "v":
                 nc.vector.tensor_copy(out=o, in_=i)
             else:
                 nc.scalar.copy(out=o, in_=i)
-
-        def q_first_copy(b):
-            nc.scalar.copy(
-                out=q_bf[0][:, b].rearrange("p (c i) j -> p c j i", i=2),
-                in_=q_raw[0][:].rearrange("p j (c i b) -> p b c j i", i=2, b=2)[:, b],
-            )
-
-        def q_first_quant(b):
-            cols = slice(128 * b, 128 * b + 128)
-            nc.vector.quantize_mx(
-                out=q_codes[0][:, cols].bitcast(FP8X4),
-                scales=q_scales[0][:, cols],
-                in_=q_bf[0][:, b].rearrange("p m j -> p (m j)"),
-            )
 
         def v_copy(pair):
             nc.vector.tensor_copy(
@@ -105,171 +111,148 @@ def tile_rows_a_exp_cap_gate_kernel(tc, qT, kT, t, v, og, out):
             )
 
         def quant(codes, scales, src):
-            nc.vector.quantize_mx(out=codes[:].bitcast(FP8X4), scales=scales[:], in_=src)
+            nc.vector.quantize_mx(out=codes.bitcast(FP8X4), scales=scales, in_=src)
 
         def k_quant(pair):
-            quant(k_codes[pair], k_scales[pair], k_bf[pair][:].rearrange("p r s j -> p (r s j)"))
+            quant(k_codes[pair][:], k_scales[pair][:], k_bf[pair][:].rearrange("p r s j -> p (r s j)"))
 
-        def q_quant(pair, a):
-            i = 2 * pair + a
-            quant(q_codes[i], q_scales[i], q_bf[i][:].rearrange("p b m j -> p (b m j)"))
+        def q_quant(u0, u1):
+            cols = slice(128 * u0, 128 * u1)
+            quant(q_codes[:, cols], q_scales[:, cols], q_bf[:, cols].rearrange("p m j -> p (m j)"))
 
         def v_quant(pair):
-            quant(v_codes[pair], v_scales[pair], v_bf[pair][:].rearrange("p g e j -> p (g e j)"))
+            quant(v_codes[pair][:], v_scales[pair][:], v_bf[pair][:].rearrange("p g e j -> p (g e j)"))
 
-        def scores(u, b):
-            pair, g = u // 4, u % 2
-            rows = slice(ROWS * g, ROWS * g + ROWS)
-            qi = 2 * pair + half(u)
-            qc = slice(128 * b, 128 * b + 128)
-            for r in range(4):
+        def scores(u):
+            pair = u // 4
+            qc = slice(128 * u, 128 * u + 128)
+            for g, r in [(g, r) for g in range(2) for r in range(4)]:
+                rows = slice(ROWS * g, ROWS * g + ROWS)
                 kc = slice(128 * r, 128 * r + 128)
                 nc.tensor.matmul_mx(
-                    out=score[g][b][:, r, :],
+                    out=score[g][u % 2][:, r, :],
                     lhsT=k_codes[pair][rows, kc].bitcast(FP8X4),
                     lhsT_scale=k_scales[pair][rows, kc],
-                    rhs=q_codes[qi][rows, qc].bitcast(FP8X4),
-                    rhs_scale=q_scales[qi][rows, qc],
+                    rhs=q_codes[rows, qc].bitcast(FP8X4),
+                    rhs_scale=q_scales[rows, qc],
                     start=True,
                     stop=True,
                 )
 
-        def cap(u, b):
+        def cap(u, g):
             nc.scalar.activation(
-                out=capped[u][:, b],
-                in_=score[u % 2][b][:].rearrange("p r m -> p m r"),
+                out=capped[u][:, g],
+                in_=score[g][u % 2][:].rearrange("p r m -> p m r"),
                 func=ACT.Tanh,
                 scale=1.0 / CAP,
             )
 
-        def expo(u, b0=0, b1=2):
+        def expo(u, g0=0, g1=2):
             nc.scalar.activation(
-                out=probs[u][:, 128 * b0 : 128 * b1].rearrange("p q r -> p (q r)"),
-                in_=capped[u][:, b0:b1].rearrange("p b m r -> p (b m r)"),
+                out=probs[u][:, 128 * g0 : 128 * g1].rearrange("p q r -> p (q r)"),
+                in_=capped[u][:, g0:g1].rearrange("p b m r -> p (b m r)"),
                 func=ACT.Exp,
                 scale=CAP,
             )
 
-        def weigh(u, b0=0, b1=2):
+        def weigh(u, g0=0, g1=2):
             nc.vector.tensor_tensor(
-                out=w_bf[u][:, 128 * b0 : 128 * b1],
-                in0=probs[u][:, 128 * b0 : 128 * b1],
-                in1=t_sb[:].unsqueeze(1).to_broadcast([P, 128 * (b1 - b0), 4]),
+                out=w_bf[u][:, 128 * g0 : 128 * g1],
+                in0=probs[u][:, 128 * g0 : 128 * g1],
+                in1=t_sb[:].unsqueeze(1).to_broadcast([P, 128 * (g1 - g0), 4]),
                 op=ALU.mult,
             )
 
-        def w_quant(u, b0=0, b1=2):
-            cols = slice(128 * b0, 128 * b1)
-            nc.vector.quantize_mx(
-                out=w_codes[u][:, cols].bitcast(FP8X4),
-                scales=w_scales[u][:, cols],
-                in_=w_bf[u][:, cols].rearrange("p q r -> p (q r)"),
-            )
+        def w_quant(u, g0=0, g1=2):
+            cols = slice(128 * g0, 128 * g1)
+            quant(w_codes[u][:, cols], w_scales[u][:, cols], w_bf[u][:, cols].rearrange("p q r -> p (q r)"))
 
-        def bank(u, b):
-            return y[0] if (u, b) == (7, 1) else y[u % 4]
+        def bank(u, g):
+            return y[0] if (u, g) == (7, 1) else y[u % 4]
 
-        def values(u, b0=0, b1=2):
-            pair, g = u // 4, u % 2
-            vc = slice(128 * g, 128 * g + 128)
-            for b in range(b0, b1):
-                wc = slice(128 * b, 128 * b + 128)
+        def values(u, g0=0, g1=2):
+            pair = u // 4
+            for g in range(g0, g1):
+                cols = slice(128 * g, 128 * g + 128)
                 nc.tensor.matmul_mx(
-                    out=bank(u, b)[:, b, :],
-                    lhsT=w_codes[u][:, wc].bitcast(FP8X4),
-                    lhsT_scale=w_scales[u][:, wc],
-                    rhs=v_codes[pair][:, vc].bitcast(FP8X4),
-                    rhs_scale=v_scales[pair][:, vc],
+                    out=bank(u, g)[:, g, :],
+                    lhsT=w_codes[u][:, cols].bitcast(FP8X4),
+                    lhsT_scale=w_scales[u][:, cols],
+                    rhs=v_codes[pair][:, cols].bitcast(FP8X4),
+                    rhs_scale=v_scales[pair][:, cols],
                     start=True,
                     stop=True,
                 )
 
-        def gate_view(x, units):
-            u = units[0]
-            full = x[u // 4][:]
-            if len(units) == 4:
-                return full
-            if len(units) == 2:
-                return full.rearrange("p (g a) c -> p a g c", a=2)[:, half(u)]
-            return full[:, 2 * (u % 2) + half(u)]
+        def gate_view(x, u0, u1):
+            return x[u0 // 4][:, u0 % 4 : u0 % 4 + u1 - u0].rearrange("p b g e -> p (b g e)")
 
-        def gate_tanh(units):
-            nc.scalar.activation(out=gate_view(gate_t, units), in_=gate_view(og_raw, units), func=ACT.Tanh, scale=0.5)
+        def gate_tanh(u0, u1):
+            nc.scalar.activation(out=gate_view(gt_all, u0, u1), in_=gate_view(og_all, u0, u1), func=ACT.Tanh, scale=0.5)
 
-        def gate_fin(units, eng):
+        def gate_fin(u0, u1, eng):
             if eng == "v":
                 nc.vector.tensor_scalar(
-                    out=gate_view(gate, units), in0=gate_view(gate_t, units),
+                    out=gate_view(g_all, u0, u1), in0=gate_view(gt_all, u0, u1),
                     scalar1=0.5, scalar2=0.5, op0=ALU.mult, op1=ALU.add,
                 )
             else:
                 nc.scalar.activation(
-                    out=gate_view(gate, units), in_=gate_view(gate_t, units), func=ACT.Copy, scale=0.5, bias=0.5
+                    out=gate_view(g_all, u0, u1), in_=gate_view(gt_all, u0, u1), func=ACT.Copy, scale=0.5, bias=0.5
                 )
 
-        def inv(u, b0=0, b1=2):
-            nc.vector.reciprocal(out=recip[u][:, b0:b1], in_=bank(u, b0)[:, b0:b1, E - 1 : E])
+        def inv(u, g0=0, g1=2):
+            nc.vector.reciprocal(out=recip[u][:, g0:g1], in_=bank(u, g0)[:, g0:g1, E - 1 : E])
 
-        def finish(u, b0=0, b1=2):
-            for b in range(b0, b1):
+        def finish(u, g0=0, g1=2):
+            for g in range(g0, g1):
                 nc.vector.scalar_tensor_tensor(
-                    out=res[u][:, b, :],
-                    in0=bank(u, b)[:, b, :],
-                    scalar=recip[u][:, b, :],
-                    in1=gate_view(gate, [u])[:, E * b : E * b + E],
+                    out=res[u][:, g, :],
+                    in0=bank(u, g)[:, g, :],
+                    scalar=recip[u][:, g, :],
+                    in1=g_all[u // 4][:, u % 4, g, :],
                     op0=ALU.mult,
                     op1=ALU.mult,
                 )
-            if b1 == 2:
+            if g1 == 2:
+                pair = u // 4
                 nc.sync.dma_start(
-                    out=out[head(u)].rearrange("(a m b) e -> a m (b e)", a=2, b=2)[half(u)],
-                    in_=res[u][:].rearrange("p b e -> p (b e)"),
+                    out=out[2 * pair : 2 * pair + 2, 128 * (u % 4) : 128 * (u % 4) + 128, :].rearrange("g m e -> m g e"),
+                    in_=res[u][:],
                 )
 
-        def v_rows(pair):
-            return v[2 * pair : 2 * pair + 2].rearrange("g (p j) e -> p g (j e)", j=4)
-
-        def og_rows(pair):
-            return og[2 * pair : 2 * pair + 2].rearrange("g (a m b) e -> m (g a) (b e)", a=2, b=2)
-
         with tc.manual_schedule():
-            nc.sync.dma_start(out=k_raw[0][:], in_=pair_rows(kT, 0))
-            nc.sync.dma_start(out=q_raw[0][:], in_=pair_rows(qT, 0)[:, :, 0:256])
-            nc.sync.dma_start(out=q_raw[1][:], in_=pair_rows(qT, 0)[:, :, 256:512])
-            nc.sync.dma_start(out=t_sb[:], in_=t.rearrange("(p j) o -> p (j o)", j=4))
-            nc.sync.dma_start(out=v_raw[0][:].rearrange("p g j e -> p g (j e)"), in_=v_rows(0))
-            nc.sync.dma_start(out=q_raw[2][:], in_=pair_rows(qT, 1)[:, :, 0:256])
-            nc.sync.dma_start(out=k_raw[1][:], in_=pair_rows(kT, 1))
-            nc.sync.dma_start(out=og_raw[0][:], in_=og_rows(0))
-            nc.sync.dma_start(out=q_raw[3][:], in_=pair_rows(qT, 1)[:, :, 256:512])
-            nc.sync.dma_start(out=og_raw[1][:], in_=og_rows(1))
-            nc.sync.dma_start(out=v_raw[1][:].rearrange("p g j e -> p g (j e)"), in_=v_rows(1))
+            load_k(0)
+            load_q(0)
+            load_q(1)
+            load_t()
+            load_v(0)
+            load_k(1)
+            load_q(2)
+            load_og(0)
+            load_og(1)
+            load_v(1)
             k_copy("v", 0, 0, K_SPLIT)
             k_copy("s", 0, K_SPLIT, 128)
             k_quant(0)
-            q_first_copy(0)
-            q_first_copy(1)
-            q_first_quant(0)
-            scores(0, 0)
-            q_first_quant(1)
-            scores(0, 1)
-            scores(1, 0)
-            scores(1, 1)
-            q_copy("v", 0, 1, 0, 64)
-            v_copy(0)
+            q_copy("s", 0, 1)
             q_quant(0, 1)
-            v_quant(0)
-            q_copy("v", 1, 0, 0, 64)
+            scores(0)
+            q_copy("v", 1, 2)
+            q_copy("v", 2, 4)
+            q_quant(1, 2)
+            scores(1)
+            q_quant(2, 4)
+            v_copy(0)
             cap(0, 0)
             cap(0, 1)
             expo(0, 0, 1)
-            cap(1, 0)
             expo(0, 1, 2)
+            cap(1, 0)
             cap(1, 1)
-            scores(2, 0)
-            scores(2, 1)
+            scores(2)
             weigh(0, 0, 1)
-            q_quant(1, 0)
+            v_quant(0)
             weigh(0, 1, 2)
             k_copy("v", 1, 0, 128)
             w_quant(0)
@@ -277,36 +260,33 @@ def tile_rows_a_exp_cap_gate_kernel(tc, qT, kT, t, v, og, out):
             cap(2, 0)
             expo(1)
             cap(2, 1)
-            gate_tanh([0, 1])
-            scores(3, 0)
-            scores(3, 1)
+            scores(3)
             values(0)
             weigh(1)
-            q_copy("v", 1, 1, 0, 64)
+            q_copy("v", 4, 6)
             w_quant(1)
-            q_quant(1, 1)
-            gate_fin([0, 1], "v")
+            q_quant(4, 6)
+            q_copy("v", 6, 8)
             inv(0)
             cap(3, 0)
             expo(2)
             cap(3, 1)
-            gate_tanh([2, 3])
-            scores(4, 0)
-            scores(4, 1)
+            gate_tanh(0, 4)
             values(1)
+            scores(4)
             weigh(2)
             inv(1)
-            finish(0)
+            q_quant(6, 8)
             w_quant(2)
-            finish(1)
+            gate_fin(0, 4, "v")
             v_copy(1)
-            gate_fin([2, 3], "v")
+            finish(0)
+            finish(1)
             cap(4, 0)
             expo(3)
             cap(4, 1)
-            gate_tanh([4, 5])
-            scores(5, 0)
-            scores(5, 1)
+            gate_tanh(4, 6)
+            scores(5)
             values(2)
             weigh(3)
             inv(2)
@@ -316,19 +296,17 @@ def tile_rows_a_exp_cap_gate_kernel(tc, qT, kT, t, v, og, out):
             cap(5, 0)
             expo(4)
             cap(5, 1)
-            scores(6, 0)
-            scores(6, 1)
+            scores(6)
             values(3)
             weigh(4)
             inv(3)
-            gate_fin([4, 5], "v")
+            gate_fin(4, 6, "v")
             w_quant(4)
             finish(3)
             cap(6, 0)
             expo(5)
             cap(6, 1)
-            scores(7, 0)
-            scores(7, 1)
+            scores(7)
             values(4)
             weigh(5)
             inv(4)
@@ -341,10 +319,10 @@ def tile_rows_a_exp_cap_gate_kernel(tc, qT, kT, t, v, og, out):
             values(5)
             expo(7, 0, 1)
             expo(7, 1, 2)
-            gate_tanh([6])
-            gate_tanh([7])
-            gate_fin([6], "s")
-            gate_fin([7], "s")
+            gate_tanh(6, 7)
+            gate_tanh(7, 8)
+            gate_fin(6, 7, "s")
+            gate_fin(7, 8, "s")
             weigh(6, 0, 1)
             inv(5)
             weigh(6, 1, 2)

@@ -15,8 +15,17 @@ ACT = mybir.ActivationFunctionType
 ALU = mybir.AluOpType
 
 P = 128
-ROWS = 64
-K_SPLIT = 84
+PACK = 4
+PAIR = 2
+PAIRS = H // PAIR
+ROWS = D // PACK
+TILE = 128
+TILES = NQ // TILE
+UNITS = PAIRS * TILES
+SCORE_BANKS = 2
+Y_BANKS = 4
+K_SPLIT = 64
+Q_LOADS = ((0, 1), (1, TILES), (TILES, UNITS))
 
 
 def tile_rows_a_exp_cap_gate_kernel(tc, qT, kT, t, v, og, out):
@@ -26,318 +35,307 @@ def tile_rows_a_exp_cap_gate_kernel(tc, qT, kT, t, v, og, out):
         ps = ctx.enter_context(tc.psum_pool(name="ps", bufs=1))
 
         def tiles(name, count, shape, dtype):
-            return [sb.tile(shape, dtype, name="%s%d" % (name, i), align_bytes=64) for i in range(count)]
+            return [sb.tile(shape, dtype, name="%s%d" % (name, n), align_bytes=64) for n in range(count)]
 
-        q_parts = [(0, 1), (1, 4), (4, 8)]
-        k_raw = tiles("k_raw", 2, [P, 4, N], F32)
-        q_raw = {}
-        for part in q_parts:
-            q_raw[part] = sb.tile([P, 4, 128 * (part[1] - part[0])], F32, name="q_raw%d" % part[0], align_bytes=64)
-        v_raw = tiles("v_raw", 2, [P, 2, 4, E], F32)
-        t_sb = tiles("t_sb", 1, [P, 4], F32)[0]
-        k_bf = tiles("k_bf", 2, [P, 4, 128, 4], BF16)
-        q_bf = tiles("q_bf", 1, [P, 1024, 4], BF16)[0]
-        v_bf = tiles("v_bf", 2, [P, 2, E, 4], BF16)
-        k_codes = tiles("k_codes", 2, [P, 512], U32)
-        k_scales = tiles("k_scales", 2, [P, 512], U8)
-        q_codes = tiles("q_codes", 1, [P, 1024], U32)[0]
-        q_scales = tiles("q_scales", 1, [P, 1024], U8)[0]
-        v_codes = tiles("v_codes", 2, [P, 256], U32)
-        v_scales = tiles("v_scales", 2, [P, 256], U8)
-        capped = tiles("capped", 8, [P, 2, 128, 4], F32)
-        probs = tiles("probs", 8, [P, 256, 4], F32)
-        w_bf = tiles("w_bf", 8, [P, 256, 4], BF16)
-        w_codes = tiles("w_codes", 8, [P, 256], U32)
-        w_scales = tiles("w_scales", 8, [P, 256], U8)
-        recip = tiles("recip", 8, [P, 2, 1], F32)
-        res = tiles("res", 8, [P, 2, E], F32)
-        score = [[ps.tile([P, 4, 128], F32, name="score%d%d" % (g, b)) for b in range(2)] for g in range(2)]
-        y = [ps.tile([P, 2, E], F32, name="y%d" % i) for i in range(4)]
+        k_raw = tiles("k_raw", PAIRS, [P, PACK, N], F32)
+        q_raw = [tiles("q_raw%d_" % u0, 1, [P, PACK, TILE * (u1 - u0)], F32)[0] for u0, u1 in Q_LOADS]
+        v_raw = tiles("v_raw", PAIRS, [P, PAIR, PACK, E], F32)
+        og_raw = tiles("og_raw", PAIRS, [P, PAIR, TILES, E], F32)
+        t_sb = tiles("t_sb", 1, [P, PACK], F32)[0]
+        k_bf = tiles("k_bf", PAIRS, [P, PACK, TILE, PACK], BF16)
+        q_bf = tiles("q_bf", 1, [P, UNITS * TILE, PACK], BF16)[0]
+        v_bf = tiles("v_bf", PAIRS, [P, PAIR, E, PACK], BF16)
+        k_codes = tiles("k_codes", PAIRS, [P, N], U32)
+        k_scales = tiles("k_scales", PAIRS, [P, N], U8)
+        q_codes = tiles("q_codes", 1, [P, UNITS * TILE], U32)[0]
+        q_scales = tiles("q_scales", 1, [P, UNITS * TILE], U8)[0]
+        v_codes = tiles("v_codes", PAIRS, [P, PAIR * E], U32)
+        v_scales = tiles("v_scales", PAIRS, [P, PAIR * E], U8)
+        capped = tiles("capped", UNITS, [P, PAIR, TILE, PACK], F32)
+        probs = tiles("probs", UNITS, [P, PAIR * TILE, PACK], F32)
+        w_bf = tiles("w_bf", UNITS, [P, PAIR * TILE, PACK], BF16)
+        w_codes = tiles("w_codes", UNITS, [P, PAIR * TILE], U32)
+        w_scales = tiles("w_scales", UNITS, [P, PAIR * TILE], U8)
+        gate_tanh = tiles("gate_tanh", PAIRS, [P, PAIR, TILES, E], F32)
+        gate = tiles("gate", PAIRS, [P, PAIR, TILES, E], F32)
+        recip = tiles("recip", UNITS, [P, PAIR, 1], F32)
+        result = tiles("result", UNITS, [P, PAIR, E], F32)
+        score = [
+            [ps.tile([P, PACK, TILE], F32, name="score%d%d" % (g, n)) for n in range(SCORE_BANKS)]
+            for g in range(PAIR)
+        ]
+        y = [ps.tile([P, PAIR, E], F32, name="y%d" % n) for n in range(Y_BANKS)]
 
-        def pair_rows(x, pair):
-            return x[2 * pair : 2 * pair + 2].rearrange("g (p j) n -> (g p) j n", j=4)
+        def cols(c0, c1):
+            return slice(TILE * c0, TILE * c1)
+
+        def heads(x, pair):
+            return x[PAIR * pair : PAIR * pair + PAIR]
+
+        def feature_rows(x, pair):
+            return heads(x, pair).rearrange("g (p j) n -> (g p) j n", j=PACK)
 
         def load_k(pair):
-            nc.sync.dma_start(out=k_raw[pair][:], in_=pair_rows(kT, pair))
+            nc.sync.dma_start(out=k_raw[pair][:], in_=feature_rows(kT, pair))
 
-        def load_q(i):
-            u0, u1 = q_parts[i]
-            c0 = 128 * (u0 % 4)
-            nc.sync.dma_start(out=q_raw[q_parts[i]][:], in_=pair_rows(qT, u0 // 4)[:, :, c0 : c0 + 128 * (u1 - u0)])
-
-        def load_t():
-            nc.sync.dma_start(out=t_sb[:], in_=t.rearrange("(p j) o -> p (j o)", j=4))
+        def load_q(n):
+            u0, u1 = Q_LOADS[n]
+            first = u0 % TILES
+            nc.sync.dma_start(out=q_raw[n][:], in_=feature_rows(qT, u0 // TILES)[:, :, cols(first, first + u1 - u0)])
 
         def load_v(pair):
             nc.sync.dma_start(
-                out=v_raw[pair][:].rearrange("p g j e -> p g (j e)"),
-                in_=v[2 * pair : 2 * pair + 2].rearrange("g (p j) e -> p g (j e)", j=4),
+                out=v_raw[pair][:].rearrange("s g j e -> s g (j e)"),
+                in_=heads(v, pair).rearrange("g (s j) e -> s g (j e)", j=PACK),
             )
 
         def load_og(pair):
-            for g in range(2):
-                nc.sync.dma_start(
-                    out=og_all[pair][:, :, g, :],
-                    in_=og[2 * pair + g].rearrange("(b m) e -> m b e", b=4),
-                )
-
-        og_all = tiles("og_all", 2, [P, 4, 2, E], F32)
-        gt_all = tiles("gt_all", 2, [P, 4, 2, E], F32)
-        g_all = tiles("g_all", 2, [P, 4, 2, E], F32)
-
-        def k_copy(eng, pair, s0, s1):
-            o = k_bf[pair][:].rearrange("p (u x) s j -> p u s j x", x=2)[:, :, s0:s1]
-            i = k_raw[pair][:].rearrange("p j (s u x) -> p u s j x", u=2, x=2)[:, :, s0:s1]
-            if eng == "v":
-                nc.vector.tensor_copy(out=o, in_=i)
-            else:
-                for u in range(2):
-                    nc.scalar.activation(out=o[:, u], in_=i[:, u], func=ACT.Copy)
-
-        def q_copy(eng, u0, u1):
-            part = [x for x in q_parts if x[0] <= u0 and u1 <= x[1]][0]
-            src = q_raw[part][:, :, 128 * (u0 - part[0]) : 128 * (u1 - part[0])]
-            o = q_bf[:, 128 * u0 : 128 * u1].rearrange("p (c i) j -> p c j i", i=4)
-            i = src.rearrange("p j (c i) -> p c j i", i=4)
-            if eng == "v":
-                nc.vector.tensor_copy(out=o, in_=i)
-            else:
-                nc.scalar.copy(out=o, in_=i)
-
-        def v_copy(pair):
-            nc.vector.tensor_copy(
-                out=v_bf[pair][:].rearrange("p g (c i) j -> p g c j i", i=4),
-                in_=v_raw[pair][:].rearrange("p g j (c i) -> p g c j i", i=4),
+            nc.sync.dma_start(
+                out=og_raw[pair][:].rearrange("m g b e -> m (g b) e"),
+                in_=heads(og, pair).rearrange("g (b m) e -> m (g b) e", b=TILES),
             )
 
-        def quant(codes, scales, src):
-            nc.vector.quantize_mx(out=codes.bitcast(FP8X4), scales=scales, in_=src)
+        def k_views(pair, s0, s1):
+            dst = k_bf[pair][:].rearrange("p (z x) s j -> p z s j x", x=2)[:, :, s0:s1]
+            src = k_raw[pair][:].rearrange("p j (s z x) -> p z s j x", z=2, x=2)[:, :, s0:s1]
+            return dst, src
 
-        def k_quant(pair):
-            quant(k_codes[pair][:], k_scales[pair][:], k_bf[pair][:].rearrange("p r s j -> p (r s j)"))
+        def round_k(pair, s0, s1):
+            dst, src = k_views(pair, s0, s1)
+            nc.vector.tensor_copy(out=dst, in_=src)
 
-        def q_quant(u0, u1):
-            cols = slice(128 * u0, 128 * u1)
-            quant(q_codes[:, cols], q_scales[:, cols], q_bf[:, cols].rearrange("p m j -> p (m j)"))
+        def round_k_on_scalar(pair, s0, s1):
+            dst, src = k_views(pair, s0, s1)
+            for z in range(2):
+                nc.scalar.activation(out=dst[:, z], in_=src[:, z], func=ACT.Copy)
 
-        def v_quant(pair):
-            quant(v_codes[pair][:], v_scales[pair][:], v_bf[pair][:].rearrange("p g e j -> p (g e j)"))
+        def round_q(u0, u1):
+            n = [lo <= u0 < hi for lo, hi in Q_LOADS].index(True)
+            first = u0 - Q_LOADS[n][0]
+            nc.vector.tensor_copy(
+                out=q_bf[:, cols(u0, u1)].rearrange("p (c i) j -> p c j i", i=4),
+                in_=q_raw[n][:, :, cols(first, first + u1 - u0)].rearrange("p j (c i) -> p c j i", i=4),
+            )
+
+        def round_v(pair):
+            nc.vector.tensor_copy(
+                out=v_bf[pair][:].rearrange("s g (c i) j -> s g c j i", i=4),
+                in_=v_raw[pair][:].rearrange("s g j (c i) -> s g c j i", i=4),
+            )
+
+        def quantize(codes, scales, values):
+            nc.vector.quantize_mx(out=codes.bitcast(FP8X4), scales=scales, in_=values)
+
+        def quantize_k(pair, r0, r1):
+            c = cols(r0, r1)
+            quantize(k_codes[pair][:, c], k_scales[pair][:, c], k_bf[pair][:, r0:r1].rearrange("p r s j -> p (r s j)"))
+
+        def quantize_q(u0, u1):
+            c = cols(u0, u1)
+            quantize(q_codes[:, c], q_scales[:, c], q_bf[:, c].rearrange("p m j -> p (m j)"))
+
+        def quantize_v(pair):
+            quantize(v_codes[pair][:], v_scales[pair][:], v_bf[pair][:].rearrange("s g e j -> s (g e j)"))
 
         def scores(u):
-            pair = u // 4
-            qc = slice(128 * u, 128 * u + 128)
-            for g, r in [(g, r) for g in range(2) for r in range(4)]:
+            pair = u // TILES
+            for g in range(PAIR):
                 rows = slice(ROWS * g, ROWS * g + ROWS)
-                kc = slice(128 * r, 128 * r + 128)
-                nc.tensor.matmul_mx(
-                    out=score[g][u % 2][:, r, :],
-                    lhsT=k_codes[pair][rows, kc].bitcast(FP8X4),
-                    lhsT_scale=k_scales[pair][rows, kc],
-                    rhs=q_codes[rows, qc].bitcast(FP8X4),
-                    rhs_scale=q_scales[rows, qc],
-                    start=True,
-                    stop=True,
-                )
+                for r in range(PACK):
+                    nc.tensor.matmul_mx(
+                        out=score[g][u % SCORE_BANKS][:, r, :],
+                        lhsT=k_codes[pair][rows, cols(r, r + 1)].bitcast(FP8X4),
+                        lhsT_scale=k_scales[pair][rows, cols(r, r + 1)],
+                        rhs=q_codes[rows, cols(u, u + 1)].bitcast(FP8X4),
+                        rhs_scale=q_scales[rows, cols(u, u + 1)],
+                        start=True,
+                        stop=True,
+                    )
 
         def cap(u, g):
             nc.scalar.activation(
                 out=capped[u][:, g],
-                in_=score[g][u % 2][:].rearrange("p r m -> p m r"),
+                in_=score[g][u % SCORE_BANKS][:].rearrange("s r m -> s m r"),
                 func=ACT.Tanh,
                 scale=1.0 / CAP,
             )
 
-        def expo(u, g0=0, g1=2):
+        def exponential(u, g0=0, g1=PAIR):
             nc.scalar.activation(
-                out=probs[u][:, 128 * g0 : 128 * g1].rearrange("p q r -> p (q r)"),
-                in_=capped[u][:, g0:g1].rearrange("p b m r -> p (b m r)"),
+                out=probs[u][:, cols(g0, g1)].rearrange("s m r -> s (m r)"),
+                in_=capped[u][:, g0:g1].rearrange("s g m r -> s (g m r)"),
                 func=ACT.Exp,
                 scale=CAP,
             )
 
-        def weigh(u, g0=0, g1=2):
+        def weigh(u, g0=0, g1=PAIR):
             nc.vector.tensor_tensor(
-                out=w_bf[u][:, 128 * g0 : 128 * g1],
-                in0=probs[u][:, 128 * g0 : 128 * g1],
-                in1=t_sb[:].unsqueeze(1).to_broadcast([P, 128 * (g1 - g0), 4]),
+                out=w_bf[u][:, cols(g0, g1)],
+                in0=probs[u][:, cols(g0, g1)],
+                in1=t_sb[:].unsqueeze(1).to_broadcast([P, TILE * (g1 - g0), PACK]),
                 op=ALU.mult,
             )
 
-        def w_quant(u, g0=0, g1=2):
-            cols = slice(128 * g0, 128 * g1)
-            quant(w_codes[u][:, cols], w_scales[u][:, cols], w_bf[u][:, cols].rearrange("p q r -> p (q r)"))
+        def quantize_w(u, g0=0, g1=PAIR):
+            c = cols(g0, g1)
+            quantize(w_codes[u][:, c], w_scales[u][:, c], w_bf[u][:, c].rearrange("s m r -> s (m r)"))
 
-        def bank(u, g):
-            return y[0] if (u, g) == (7, 1) else y[u % 4]
+        def y_bank(u, g):
+            is_last = (u, g) == (UNITS - 1, PAIR - 1)
+            return y[(u + 1) % Y_BANKS] if is_last else y[u % Y_BANKS]
 
-        def values(u, g0=0, g1=2):
-            pair = u // 4
+        def mix_values(u, g0=0, g1=PAIR):
+            pair = u // TILES
             for g in range(g0, g1):
-                cols = slice(128 * g, 128 * g + 128)
                 nc.tensor.matmul_mx(
-                    out=bank(u, g)[:, g, :],
-                    lhsT=w_codes[u][:, cols].bitcast(FP8X4),
-                    lhsT_scale=w_scales[u][:, cols],
-                    rhs=v_codes[pair][:, cols].bitcast(FP8X4),
-                    rhs_scale=v_scales[pair][:, cols],
+                    out=y_bank(u, g)[:, g, :],
+                    lhsT=w_codes[u][:, cols(g, g + 1)].bitcast(FP8X4),
+                    lhsT_scale=w_scales[u][:, cols(g, g + 1)],
+                    rhs=v_codes[pair][:, cols(g, g + 1)].bitcast(FP8X4),
+                    rhs_scale=v_scales[pair][:, cols(g, g + 1)],
                     start=True,
                     stop=True,
                 )
 
-        def gate_view(x, u0, u1):
-            return x[u0 // 4][:, u0 % 4 : u0 % 4 + u1 - u0].rearrange("p b g e -> p (b g e)")
+        def of_units(x, u0, u1):
+            first = u0 % TILES
+            return x[u0 // TILES][:, :, first : first + u1 - u0].rearrange("m g b e -> m g (b e)")
 
-        def gate_tanh(u0, u1):
-            nc.scalar.activation(out=gate_view(gt_all, u0, u1), in_=gate_view(og_all, u0, u1), func=ACT.Tanh, scale=0.5)
+        def gate_first_half(u0, u1):
+            nc.scalar.activation(
+                out=of_units(gate_tanh, u0, u1), in_=of_units(og_raw, u0, u1), func=ACT.Tanh, scale=0.5
+            )
 
-        def gate_fin(u0, u1, eng):
-            if eng == "v":
-                nc.vector.tensor_scalar(
-                    out=gate_view(g_all, u0, u1), in0=gate_view(gt_all, u0, u1),
-                    scalar1=0.5, scalar2=0.5, op0=ALU.mult, op1=ALU.add,
-                )
-            else:
-                nc.scalar.activation(
-                    out=gate_view(g_all, u0, u1), in_=gate_view(gt_all, u0, u1), func=ACT.Copy, scale=0.5, bias=0.5
-                )
+        def gate_second_half(u0, u1):
+            nc.vector.tensor_scalar(
+                out=of_units(gate, u0, u1),
+                in0=of_units(gate_tanh, u0, u1),
+                scalar1=0.5,
+                scalar2=0.5,
+                op0=ALU.mult,
+                op1=ALU.add,
+            )
 
-        def inv(u, g0=0, g1=2):
-            nc.vector.reciprocal(out=recip[u][:, g0:g1], in_=bank(u, g0)[:, g0:g1, E - 1 : E])
+        def gate_second_half_on_scalar(u0, u1):
+            nc.scalar.activation(
+                out=of_units(gate, u0, u1), in_=of_units(gate_tanh, u0, u1), func=ACT.Copy, scale=0.5, bias=0.5
+            )
 
-        def finish(u, g0=0, g1=2):
-            for g in range(g0, g1):
+        def invert(u, g0=0, g1=PAIR):
+            nc.vector.reciprocal(out=recip[u][:, g0:g1], in_=y_bank(u, g0)[:, g0:g1, E - 1 : E])
+
+        def finish(u):
+            pair, b = divmod(u, TILES)
+            for g in range(PAIR):
                 nc.vector.scalar_tensor_tensor(
-                    out=res[u][:, g, :],
-                    in0=bank(u, g)[:, g, :],
+                    out=result[u][:, g, :],
+                    in0=y_bank(u, g)[:, g, :],
                     scalar=recip[u][:, g, :],
-                    in1=g_all[u // 4][:, u % 4, g, :],
+                    in1=gate[pair][:, g, b, :],
                     op0=ALU.mult,
                     op1=ALU.mult,
                 )
-            if g1 == 2:
-                pair = u // 4
-                nc.sync.dma_start(
-                    out=out[2 * pair : 2 * pair + 2, 128 * (u % 4) : 128 * (u % 4) + 128, :].rearrange("g m e -> m g e"),
-                    in_=res[u][:],
-                )
+            nc.sync.dma_start(out=heads(out, pair)[:, cols(b, b + 1), :].rearrange("g m e -> m g e"), in_=result[u][:])
 
         with tc.manual_schedule():
             load_k(0)
             load_q(0)
             load_q(1)
-            load_t()
+            nc.sync.dma_start(out=t_sb[:], in_=t.rearrange("(s r) o -> s (r o)", r=PACK))
             load_v(0)
             load_k(1)
             load_q(2)
             load_og(0)
             load_og(1)
             load_v(1)
-            k_copy("v", 0, 0, K_SPLIT)
-            k_copy("s", 0, K_SPLIT, 128)
-            k_quant(0)
-            q_copy("s", 0, 1)
-            q_quant(0, 1)
+
+            round_k(0, 0, K_SPLIT)
+            round_k_on_scalar(0, K_SPLIT, TILE)
+            round_q(0, 1)
+            quantize_k(0, 0, 2)
+            quantize_q(0, 1)
+            quantize_k(0, 2, PACK)
             scores(0)
-            q_copy("v", 1, 2)
-            q_copy("v", 2, 4)
-            q_quant(1, 2)
+            round_q(1, 2)
+            round_q(2, TILES)
+            quantize_q(1, 2)
             scores(1)
-            q_quant(2, 4)
-            v_copy(0)
-            cap(0, 0)
-            cap(0, 1)
-            expo(0, 0, 1)
-            expo(0, 1, 2)
-            cap(1, 0)
-            cap(1, 1)
+            quantize_q(2, TILES)
+            round_v(0)
+
+            for g in range(PAIR):
+                cap(0, g)
+            for g in range(PAIR):
+                exponential(0, g, g + 1)
+            for g in range(PAIR):
+                cap(1, g)
             scores(2)
             weigh(0, 0, 1)
-            v_quant(0)
+            quantize_v(0)
             weigh(0, 1, 2)
-            k_copy("v", 1, 0, 128)
-            w_quant(0)
-            k_quant(1)
-            cap(2, 0)
-            expo(1)
-            cap(2, 1)
-            scores(3)
-            values(0)
-            weigh(1)
-            q_copy("v", 4, 6)
-            w_quant(1)
-            q_quant(4, 6)
-            q_copy("v", 6, 8)
-            inv(0)
-            cap(3, 0)
-            expo(2)
-            cap(3, 1)
-            gate_tanh(0, 4)
-            values(1)
-            scores(4)
-            weigh(2)
-            inv(1)
-            q_quant(6, 8)
-            w_quant(2)
-            gate_fin(0, 4, "v")
-            v_copy(1)
-            finish(0)
-            finish(1)
-            cap(4, 0)
-            expo(3)
-            cap(4, 1)
-            gate_tanh(4, 6)
-            scores(5)
-            values(2)
-            weigh(3)
-            inv(2)
-            v_quant(1)
-            w_quant(3)
-            finish(2)
-            cap(5, 0)
-            expo(4)
-            cap(5, 1)
-            scores(6)
-            values(3)
-            weigh(4)
-            inv(3)
-            gate_fin(4, 6, "v")
-            w_quant(4)
-            finish(3)
-            cap(6, 0)
-            expo(5)
-            cap(6, 1)
-            scores(7)
-            values(4)
-            weigh(5)
-            inv(4)
-            w_quant(5)
-            finish(4)
-            expo(6, 0, 1)
-            cap(7, 0)
-            expo(6, 1, 2)
-            cap(7, 1)
-            values(5)
-            expo(7, 0, 1)
-            expo(7, 1, 2)
-            gate_tanh(6, 7)
-            gate_tanh(7, 8)
-            gate_fin(6, 7, "s")
-            gate_fin(7, 8, "s")
-            weigh(6, 0, 1)
-            inv(5)
-            weigh(6, 1, 2)
-            finish(5)
-            w_quant(6)
-            values(6)
-            weigh(7, 0, 1)
-            weigh(7, 1, 2)
-            w_quant(7, 0, 1)
-            values(7, 0, 1)
-            inv(6)
-            w_quant(7, 1, 2)
-            values(7, 1, 2)
-            finish(6)
-            inv(7, 0, 1)
-            inv(7, 1, 2)
-            finish(7, 0, 1)
-            finish(7, 1, 2)
+            round_k(1, 0, TILE)
+            quantize_w(0)
+            quantize_k(1, 0, PACK)
+
+            middle = TILES + TILES // 2
+            for u in range(1, middle):
+                cap(u + 1, 0)
+                exponential(u)
+                cap(u + 1, 1)
+                if u == 2:
+                    gate_first_half(0, TILES)
+                if u == 3:
+                    gate_first_half(TILES, middle)
+                scores(u + 2)
+                mix_values(u - 1)
+                weigh(u)
+                if u == 1:
+                    round_q(TILES, middle)
+                    quantize_w(u)
+                    quantize_q(TILES, middle)
+                    round_q(middle, UNITS)
+                elif u == 2:
+                    quantize_q(middle, UNITS)
+                    quantize_w(u)
+                    round_v(1)
+                    gate_second_half(0, TILES)
+                    invert(0)
+                    invert(1)
+                    quantize_v(1)
+                    finish(0)
+                else:
+                    finish(u - 2)
+                    quantize_w(u)
+                    invert(u - 1)
+                if u == 3:
+                    gate_second_half(TILES, middle)
+
+            before, last = UNITS - 2, UNITS - 1
+            for g in range(PAIR):
+                exponential(before, g, g + 1)
+                cap(last, g)
+            mix_values(before - 1)
+            for g in range(PAIR):
+                exponential(last, g, g + 1)
+            for u in (before, last):
+                gate_first_half(u, u + 1)
+            for u in (before, last):
+                gate_second_half_on_scalar(u, u + 1)
+            weigh(before, 0, 1)
+            finish(before - 2)
+            weigh(before, 1, 2)
+            invert(before - 1)
+            weigh(last, 0, 1)
+            quantize_w(before)
+            mix_values(before)
+            finish(before - 1)
+            weigh(last, 1, 2)
+            quantize_w(last, 0, 1)
+            mix_values(last, 0, 1)
+            invert(before)
+            quantize_w(last, 1, 2)
+            mix_values(last, 1, 2)
+            finish(before)
+            invert(last, 0, 1)
+            invert(last, 1, 2)
+            finish(last)

from contextlib import ExitStack

import concourse.mybir as mybir

H, D, NQ, N, E = 4, 256, 512, 512, 128
CAP = 2.0
FLOPS = 2 * H * NQ * N * (D + E)

F32 = mybir.dt.float32
BF16 = mybir.dt.bfloat16
U32 = mybir.dt.uint32
U8 = mybir.dt.uint8
FP8X4 = mybir.dt.float8_e4m3fn_x4
ACT = mybir.ActivationFunctionType
ALU = mybir.AluOpType

P = 128
PACK = 4
PAIR = 2
PAIRS = H // PAIR
ROWS = D // PACK
TILE = 128
TILES = NQ // TILE
UNITS = PAIRS * TILES
SCORE_BANKS = 2
Y_BANKS = 4
K_SPLIT = 64
Q_LOADS = ((0, 1), (1, TILES), (TILES, UNITS))


def tile_rows_a_exp_cap_gate_kernel(tc, qT, kT, t, v, og, out):
    nc = tc.nc
    with ExitStack() as ctx:
        sb = ctx.enter_context(tc.tile_pool(name="sb", bufs=1))
        ps = ctx.enter_context(tc.psum_pool(name="ps", bufs=1))

        def tiles(name, count, shape, dtype):
            return [sb.tile(shape, dtype, name="%s%d" % (name, n), align_bytes=64) for n in range(count)]

        k_raw = tiles("k_raw", PAIRS, [P, PACK, N], F32)
        q_raw = [tiles("q_raw%d_" % u0, 1, [P, PACK, TILE * (u1 - u0)], F32)[0] for u0, u1 in Q_LOADS]
        v_raw = tiles("v_raw", PAIRS, [P, PAIR, PACK, E], F32)
        og_raw = tiles("og_raw", PAIRS, [P, PAIR, TILES, E], F32)
        t_sb = tiles("t_sb", 1, [P, PACK], F32)[0]
        k_bf = tiles("k_bf", PAIRS, [P, PACK, TILE, PACK], BF16)
        q_bf = tiles("q_bf", 1, [P, UNITS * TILE, PACK], BF16)[0]
        v_bf = tiles("v_bf", PAIRS, [P, PAIR, E, PACK], BF16)
        k_codes = tiles("k_codes", PAIRS, [P, N], U32)
        k_scales = tiles("k_scales", PAIRS, [P, N], U8)
        q_codes = tiles("q_codes", 1, [P, UNITS * TILE], U32)[0]
        q_scales = tiles("q_scales", 1, [P, UNITS * TILE], U8)[0]
        v_codes = tiles("v_codes", PAIRS, [P, PAIR * E], U32)
        v_scales = tiles("v_scales", PAIRS, [P, PAIR * E], U8)
        capped = tiles("capped", UNITS, [P, PAIR, TILE, PACK], F32)
        probs = tiles("probs", UNITS, [P, PAIR * TILE, PACK], F32)
        w_bf = tiles("w_bf", UNITS, [P, PAIR * TILE, PACK], BF16)
        w_codes = tiles("w_codes", UNITS, [P, PAIR * TILE], U32)
        w_scales = tiles("w_scales", UNITS, [P, PAIR * TILE], U8)
        gate_tanh = tiles("gate_tanh", PAIRS, [P, PAIR, TILES, E], F32)
        gate = tiles("gate", PAIRS, [P, PAIR, TILES, E], F32)
        recip = tiles("recip", UNITS, [P, PAIR, 1], F32)
        result = tiles("result", UNITS, [P, PAIR, E], F32)
        score = [
            [ps.tile([P, PACK, TILE], F32, name="score%d%d" % (g, n)) for n in range(SCORE_BANKS)]
            for g in range(PAIR)
        ]
        y = [ps.tile([P, PAIR, E], F32, name="y%d" % n) for n in range(Y_BANKS)]

        def cols(c0, c1):
            return slice(TILE * c0, TILE * c1)

        def heads(x, pair):
            return x[PAIR * pair : PAIR * pair + PAIR]

        def feature_rows(x, pair):
            return heads(x, pair).rearrange("g (p j) n -> (g p) j n", j=PACK)

        def load_k(pair):
            nc.sync.dma_start(out=k_raw[pair][:], in_=feature_rows(kT, pair))

        def load_q(n):
            u0, u1 = Q_LOADS[n]
            first = u0 % TILES
            nc.sync.dma_start(out=q_raw[n][:], in_=feature_rows(qT, u0 // TILES)[:, :, cols(first, first + u1 - u0)])

        def load_v(pair):
            nc.sync.dma_start(
                out=v_raw[pair][:].rearrange("s g j e -> s g (j e)"),
                in_=heads(v, pair).rearrange("g (s j) e -> s g (j e)", j=PACK),
            )

        def load_og(pair):
            nc.sync.dma_start(
                out=og_raw[pair][:].rearrange("m g b e -> m (g b) e"),
                in_=heads(og, pair).rearrange("g (b m) e -> m (g b) e", b=TILES),
            )

        def k_views(pair, s0, s1):
            dst = k_bf[pair][:].rearrange("p (z x) s j -> p z s j x", x=2)[:, :, s0:s1]
            src = k_raw[pair][:].rearrange("p j (s z x) -> p z s j x", z=2, x=2)[:, :, s0:s1]
            return dst, src

        def round_k(pair, s0, s1):
            dst, src = k_views(pair, s0, s1)
            nc.vector.tensor_copy(out=dst, in_=src)

        def round_k_on_scalar(pair, s0, s1):
            dst, src = k_views(pair, s0, s1)
            for z in range(2):
                nc.scalar.activation(out=dst[:, z], in_=src[:, z], func=ACT.Copy)

        def round_q(u0, u1):
            n = [lo <= u0 < hi for lo, hi in Q_LOADS].index(True)
            first = u0 - Q_LOADS[n][0]
            nc.vector.tensor_copy(
                out=q_bf[:, cols(u0, u1)].rearrange("p (c i) j -> p c j i", i=4),
                in_=q_raw[n][:, :, cols(first, first + u1 - u0)].rearrange("p j (c i) -> p c j i", i=4),
            )

        def round_v(pair):
            nc.vector.tensor_copy(
                out=v_bf[pair][:].rearrange("s g (c i) j -> s g c j i", i=4),
                in_=v_raw[pair][:].rearrange("s g j (c i) -> s g c j i", i=4),
            )

        def quantize(codes, scales, values):
            nc.vector.quantize_mx(out=codes.bitcast(FP8X4), scales=scales, in_=values)

        def quantize_k(pair, r0, r1):
            c = cols(r0, r1)
            quantize(k_codes[pair][:, c], k_scales[pair][:, c], k_bf[pair][:, r0:r1].rearrange("p r s j -> p (r s j)"))

        def quantize_q(u0, u1):
            c = cols(u0, u1)
            quantize(q_codes[:, c], q_scales[:, c], q_bf[:, c].rearrange("p m j -> p (m j)"))

        def quantize_v(pair):
            quantize(v_codes[pair][:], v_scales[pair][:], v_bf[pair][:].rearrange("s g e j -> s (g e j)"))

        def scores(u):
            pair = u // TILES
            for g in range(PAIR):
                rows = slice(ROWS * g, ROWS * g + ROWS)
                for r in range(PACK):
                    nc.tensor.matmul_mx(
                        out=score[g][u % SCORE_BANKS][:, r, :],
                        lhsT=k_codes[pair][rows, cols(r, r + 1)].bitcast(FP8X4),
                        lhsT_scale=k_scales[pair][rows, cols(r, r + 1)],
                        rhs=q_codes[rows, cols(u, u + 1)].bitcast(FP8X4),
                        rhs_scale=q_scales[rows, cols(u, u + 1)],
                        start=True,
                        stop=True,
                    )

        def cap(u, g):
            nc.scalar.activation(
                out=capped[u][:, g],
                in_=score[g][u % SCORE_BANKS][:].rearrange("s r m -> s m r"),
                func=ACT.Tanh,
                scale=1.0 / CAP,
            )

        def exponential(u, g0=0, g1=PAIR):
            nc.scalar.activation(
                out=probs[u][:, cols(g0, g1)].rearrange("s m r -> s (m r)"),
                in_=capped[u][:, g0:g1].rearrange("s g m r -> s (g m r)"),
                func=ACT.Exp,
                scale=CAP,
            )

        def weigh(u, g0=0, g1=PAIR):
            nc.vector.tensor_tensor(
                out=w_bf[u][:, cols(g0, g1)],
                in0=probs[u][:, cols(g0, g1)],
                in1=t_sb[:].unsqueeze(1).to_broadcast([P, TILE * (g1 - g0), PACK]),
                op=ALU.mult,
            )

        def quantize_w(u, g0=0, g1=PAIR):
            c = cols(g0, g1)
            quantize(w_codes[u][:, c], w_scales[u][:, c], w_bf[u][:, c].rearrange("s m r -> s (m r)"))

        def y_bank(u, g):
            is_last = (u, g) == (UNITS - 1, PAIR - 1)
            return y[(u + 1) % Y_BANKS] if is_last else y[u % Y_BANKS]

        def mix_values(u, g0=0, g1=PAIR):
            pair = u // TILES
            for g in range(g0, g1):
                nc.tensor.matmul_mx(
                    out=y_bank(u, g)[:, g, :],
                    lhsT=w_codes[u][:, cols(g, g + 1)].bitcast(FP8X4),
                    lhsT_scale=w_scales[u][:, cols(g, g + 1)],
                    rhs=v_codes[pair][:, cols(g, g + 1)].bitcast(FP8X4),
                    rhs_scale=v_scales[pair][:, cols(g, g + 1)],
                    start=True,
                    stop=True,
                )

        def of_units(x, u0, u1):
            first = u0 % TILES
            return x[u0 // TILES][:, :, first : first + u1 - u0].rearrange("m g b e -> m g (b e)")

        def gate_first_half(u0, u1):
            nc.scalar.activation(
                out=of_units(gate_tanh, u0, u1), in_=of_units(og_raw, u0, u1), func=ACT.Tanh, scale=0.5
            )

        def gate_second_half(u0, u1):
            nc.vector.tensor_scalar(
                out=of_units(gate, u0, u1),
                in0=of_units(gate_tanh, u0, u1),
                scalar1=0.5,
                scalar2=0.5,
                op0=ALU.mult,
                op1=ALU.add,
            )

        def gate_second_half_on_scalar(u0, u1):
            nc.scalar.activation(
                out=of_units(gate, u0, u1), in_=of_units(gate_tanh, u0, u1), func=ACT.Copy, scale=0.5, bias=0.5
            )

        def invert(u, g0=0, g1=PAIR):
            nc.vector.reciprocal(out=recip[u][:, g0:g1], in_=y_bank(u, g0)[:, g0:g1, E - 1 : E])

        def finish(u):
            pair, b = divmod(u, TILES)
            for g in range(PAIR):
                nc.vector.scalar_tensor_tensor(
                    out=result[u][:, g, :],
                    in0=y_bank(u, g)[:, g, :],
                    scalar=recip[u][:, g, :],
                    in1=gate[pair][:, g, b, :],
                    op0=ALU.mult,
                    op1=ALU.mult,
                )
            nc.sync.dma_start(out=heads(out, pair)[:, cols(b, b + 1), :].rearrange("g m e -> m g e"), in_=result[u][:])

        with tc.manual_schedule():
            load_k(0)
            load_q(0)
            load_q(1)
            nc.sync.dma_start(out=t_sb[:], in_=t.rearrange("(s r) o -> s (r o)", r=PACK))
            load_v(0)
            load_k(1)
            load_q(2)
            load_og(0)
            load_og(1)
            load_v(1)

            round_k(0, 0, K_SPLIT)
            round_k_on_scalar(0, K_SPLIT, TILE)
            round_q(0, 1)
            quantize_k(0, 0, 2)
            quantize_q(0, 1)
            quantize_k(0, 2, PACK)
            scores(0)
            round_q(1, 2)
            round_q(2, TILES)
            quantize_q(1, 2)
            scores(1)
            quantize_q(2, TILES)
            round_v(0)

            for g in range(PAIR):
                cap(0, g)
            for g in range(PAIR):
                exponential(0, g, g + 1)
            for g in range(PAIR):
                cap(1, g)
            scores(2)
            weigh(0, 0, 1)
            quantize_v(0)
            weigh(0, 1, 2)
            round_k(1, 0, TILE)
            quantize_w(0)
            quantize_k(1, 0, PACK)

            middle = TILES + TILES // 2
            for u in range(1, middle):
                cap(u + 1, 0)
                exponential(u)
                cap(u + 1, 1)
                if u == 2:
                    gate_first_half(0, TILES)
                if u == 3:
                    gate_first_half(TILES, middle)
                scores(u + 2)
                mix_values(u - 1)
                weigh(u)
                if u == 1:
                    round_q(TILES, middle)
                    quantize_w(u)
                    quantize_q(TILES, middle)
                    round_q(middle, UNITS)
                elif u == 2:
                    quantize_q(middle, UNITS)
                    quantize_w(u)
                    round_v(1)
                    gate_second_half(0, TILES)
                    invert(0)
                    invert(1)
                    quantize_v(1)
                    finish(0)
                else:
                    finish(u - 2)
                    quantize_w(u)
                    invert(u - 1)
                if u == 3:
                    gate_second_half(TILES, middle)

            before, last = UNITS - 2, UNITS - 1
            for g in range(PAIR):
                exponential(before, g, g + 1)
                cap(last, g)
            mix_values(before - 1)
            for g in range(PAIR):
                exponential(last, g, g + 1)
            for u in (before, last):
                gate_first_half(u, u + 1)
            for u in (before, last):
                gate_second_half_on_scalar(u, u + 1)
            weigh(before, 0, 1)
            finish(before - 2)
            weigh(before, 1, 2)
            invert(before - 1)
            weigh(last, 0, 1)
            quantize_w(before)
            mix_values(before)
            finish(before - 1)
            weigh(last, 1, 2)
            quantize_w(last, 0, 1)
            mix_values(last, 0, 1)
            invert(before)
            quantize_w(last, 1, 2)
            mix_values(last, 1, 2)
            finish(before)
            invert(last, 0, 1)
            invert(last, 1, 2)
            finish(last)
